import numpy as np
import ml_dtypes

BF16 = ml_dtypes.bfloat16


def bf(x):
    return np.asarray(x, np.float32).astype(BF16)


def f32(x):
    return np.asarray(x, np.float32)


def f64(x):
    return np.asarray(x).astype(np.float64)


def striped(idx):
    return np.tile(idx.reshape(-1, 16).T, (8, 1))


def rows(idx, k):
    return np.tile(idx, (k, 1))


def look(tab, idx):
    return np.take_along_axis(f64(tab), rows(idx, len(tab)), axis=1)


K, S, V, N = 512, 2048, 512, 512


def setup_inputs():
    return {"tab": f32(np.random.standard_normal((2, K, S))), "y": f32(np.random.standard_normal((K, V))), "offs": striped(np.random.permutation(S)[:N])}


def reference(tab, y, offs):
    idx = offs[:16].T.reshape(-1)
    x = (look(tab[0], idx) - f64(y)) * (1.0 / (1.0 + np.exp(-look(tab[1], idx))))
    return x

@@ -1,0 +1,46 @@
+import concourse.mybir as mybir
+
+F32 = mybir.dt.float32
+U16 = mybir.dt.uint16
+SUBTRACT = mybir.AluOpType.subtract
+MULT = mybir.AluOpType.mult
+SIGMOID = mybir.ActivationFunctionType.Sigmoid
+
+P = 128
+
+
+def tile_lookup_vg_subsig_out_kernel(tc, tab, y, offs, out):
+    nc = tc.nc
+    rows, places = tab.shape[1], tab.shape[2]
+    entries = y.shape[1]
+    blocks = rows // P
+
+    tab_rows = tab.rearrange("t (p b) s -> t p b s", b=blocks)
+    y_rows = y.rearrange("(p b) n -> p (b n)", b=blocks)
+    out_rows = out.rearrange("(p b) n -> p b n", b=blocks)
+
+    with tc.tile_pool(name="held", bufs=1) as held:
+        offsets = held.tile([P, entries // 16], U16, name="offsets")
+        nc.sync.dma_start(offsets[:], offs)
+        stream = held.tile([P, blocks * entries], F32, name="stream")
+        nc.sync.dma_start(stream[:], y_rows)
+
+        gates = [held.tile([P, places], F32, name=f"gates{b}") for b in range(blocks)]
+        values = [held.tile([P, places], F32, name=f"values{b}") for b in range(blocks)]
+        for b in range(blocks):
+            nc.sync.dma_start(gates[b][:], tab_rows[1, :, b, :])
+            nc.sync.dma_start(values[b][:], tab_rows[0, :, b, :])
+
+        for b in range(blocks):
+            opening = held.tile([P, entries], F32, name=f"opening{b}")
+            nc.scalar.activation(opening[:], gates[b][:].indirect(offsets[:]), SIGMOID)
+            difference = held.tile([P, entries], F32, name=f"difference{b}")
+            nc.vector.tensor_tensor(
+                difference[:],
+                values[b][:].indirect(offsets[:]),
+                stream[:, b * entries : (b + 1) * entries],
+                SUBTRACT,
+            )
+            x = held.tile([P, entries], F32, name=f"x{b}")
+            nc.vector.tensor_tensor(x[:], difference[:], opening[:], MULT)
+            nc.sync.dma_start(out_rows[:, b, :], x[:])

@@ -7,6 +7,7 @@ MULT = mybir.AluOpType.mult
 SIGMOID = mybir.ActivationFunctionType.Sigmoid
 
 P = 128
+LAST_PIECES = 2
 
 
 def tile_lookup_vg_subsig_out_kernel(tc, tab, y, offs, out):
@@ -28,12 +29,10 @@ def tile_lookup_vg_subsig_out_kernel(tc, tab, y, offs, out):
         gates = [held.tile([P, places], F32, name=f"gates{b}") for b in range(blocks)]
         values = [held.tile([P, places], F32, name=f"values{b}") for b in range(blocks)]
         for b in range(blocks):
-            nc.sync.dma_start(gates[b][:], tab_rows[1, :, b, :])
             nc.sync.dma_start(values[b][:], tab_rows[0, :, b, :])
+            nc.sync.dma_start(gates[b][:], tab_rows[1, :, b, :])
 
         for b in range(blocks):
-            opening = held.tile([P, entries], F32, name=f"opening{b}")
-            nc.scalar.activation(opening[:], gates[b][:].indirect(offsets[:]), SIGMOID)
             difference = held.tile([P, entries], F32, name=f"difference{b}")
             nc.vector.tensor_tensor(
                 difference[:],
@@ -41,6 +40,13 @@ def tile_lookup_vg_subsig_out_kernel(tc, tab, y, offs, out):
                 stream[:, b * entries : (b + 1) * entries],
                 SUBTRACT,
             )
+            pieces = LAST_PIECES if b == blocks - 1 else 1
+            width = entries // pieces
+            opening = held.tile([P, entries], F32, name=f"opening{b}")
             x = held.tile([P, entries], F32, name=f"x{b}")
-            nc.vector.tensor_tensor(x[:], difference[:], opening[:], MULT)
-            nc.sync.dma_start(out_rows[:, b, :], x[:])
+            for k in range(pieces):
+                cut = slice(k * width, (k + 1) * width)
+                listed = offsets[:, k * width // 16 : (k + 1) * width // 16]
+                nc.scalar.activation(opening[:, cut], gates[b][:].indirect(listed), SIGMOID)
+                nc.vector.tensor_tensor(x[:, cut], difference[:, cut], opening[:, cut], MULT)
+                nc.sync.dma_start(out_rows[:, b, cut], x[:, cut])

import concourse.mybir as mybir

F32 = mybir.dt.float32
U16 = mybir.dt.uint16
SUBTRACT = mybir.AluOpType.subtract
MULT = mybir.AluOpType.mult
SIGMOID = mybir.ActivationFunctionType.Sigmoid

P = 128
LAST_PIECES = 2


def tile_lookup_vg_subsig_out_kernel(tc, tab, y, offs, out):
    nc = tc.nc
    rows, places = tab.shape[1], tab.shape[2]
    entries = y.shape[1]
    blocks = rows // P

    tab_rows = tab.rearrange("t (p b) s -> t p b s", b=blocks)
    y_rows = y.rearrange("(p b) n -> p (b n)", b=blocks)
    out_rows = out.rearrange("(p b) n -> p b n", b=blocks)

    with tc.tile_pool(name="held", bufs=1) as held:
        offsets = held.tile([P, entries // 16], U16, name="offsets")
        nc.sync.dma_start(offsets[:], offs)
        stream = held.tile([P, blocks * entries], F32, name="stream")
        nc.sync.dma_start(stream[:], y_rows)

        gates = [held.tile([P, places], F32, name=f"gates{b}") for b in range(blocks)]
        values = [held.tile([P, places], F32, name=f"values{b}") for b in range(blocks)]
        for b in range(blocks):
            nc.sync.dma_start(values[b][:], tab_rows[0, :, b, :])
            nc.sync.dma_start(gates[b][:], tab_rows[1, :, b, :])

        for b in range(blocks):
            difference = held.tile([P, entries], F32, name=f"difference{b}")
            nc.vector.tensor_tensor(
                difference[:],
                values[b][:].indirect(offsets[:]),
                stream[:, b * entries : (b + 1) * entries],
                SUBTRACT,
            )
            pieces = LAST_PIECES if b == blocks - 1 else 1
            width = entries // pieces
            opening = held.tile([P, entries], F32, name=f"opening{b}")
            x = held.tile([P, entries], F32, name=f"x{b}")
            for k in range(pieces):
                cut = slice(k * width, (k + 1) * width)
                listed = offsets[:, k * width // 16 : (k + 1) * width // 16]
                nc.scalar.activation(opening[:, cut], gates[b][:].indirect(listed), SIGMOID)
                nc.vector.tensor_tensor(x[:, cut], difference[:, cut], opening[:, cut], MULT)
                nc.sync.dma_start(out_rows[:, b, cut], x[:, cut])
